import numpy as np
import ml_dtypes


def mxq(x, axis, fmt="e4m3"):
    dtype, down = {"e4m3": (ml_dtypes.float8_e4m3fn, 7), "e5m2": (ml_dtypes.float8_e5m2, 14)}[fmt]
    v = np.moveaxis(np.asarray(x, np.float32).astype(ml_dtypes.bfloat16).astype(np.float64), axis, -1)
    blocks = v.reshape(v.shape[:-1] + (-1, 32))
    amax = np.abs(blocks).max(-1, keepdims=True)
    byte = np.maximum(np.where(amax > 0, np.frexp(amax)[1] - 1 + 127, 0) - down, 1)
    scale = np.exp2(byte - 127.0)
    codes = (blocks / scale).astype(np.float32).astype(dtype).astype(np.float64)
    return np.moveaxis((codes * scale).reshape(v.shape), -1, axis)


WIDE = False


def mx_kscale(k):
    if not WIDE:
        return np.ones(k)
    levels = np.array([10, -10, 5, -5, 0])
    if k % 512:
        return np.exp2(np.random.permutation(np.resize(levels, k // 32))).repeat(32)
    a = np.empty((k // 512, 16))
    for p in range(k // 512):
        a[p, :8] = np.random.permutation(np.resize(levels, 8))
        for g in range(8):
            far = levels[np.abs(levels - a[p, g]) >= 10]
            a[p, g + 8] = far[np.random.randint(len(far))]
    return np.exp2(a.ravel()).repeat(32)


def f64(x):
    return np.asarray(x).astype(np.float64)


def striped(idx):
    return np.tile(idx.reshape(-1, 16).T, (8, 1)).astype(np.uint16)


def unstriped(offs):
    return offs[:16].T.reshape(-1).astype(np.int64)


E2M1 = np.array([0.0, 0.5, 1.0, 1.5, 2.0, 3.0, 4.0, 6.0, -0.0, -0.5, -1.0, -1.5, -2.0, -3.0, -4.0, -6.0])


def pack_weight(w, fmt):
    k, n = w.shape
    w = f64(np.asarray(w, np.float32).astype(ml_dtypes.bfloat16)).reshape(k // 32, 32, n)
    amax = np.abs(w).max(1)
    if fmt == "e4m3":
        byte = np.frexp(amax)[1] - 1 + 127 - 7
    else:
        mant, ex = np.frexp(amax / 6.0)
        byte = np.where(mant > 0.5, ex, ex - 1) + 127
    byte = np.clip(np.where(amax > 0, byte, 1), 1, 254)
    scaled = (w * np.exp2(127.0 - byte)[:, None, :]).reshape(k, n).astype(np.float32)
    by_word = np.ascontiguousarray(scaled.reshape(k // 512, 128, 4, n).transpose(0, 1, 3, 2))
    if fmt == "e4m3":
        words = by_word.astype(ml_dtypes.float8_e4m3fn).view(np.uint8)
    else:
        c = by_word.astype(ml_dtypes.float4_e2m1fn).view(np.uint8) & 0xF
        words = (c[..., 0::2] | (c[..., 1::2] << 4)).reshape(k // 512, 128, 2 * n)
    return np.ascontiguousarray(words), np.ascontiguousarray(byte.astype(np.uint8).reshape(k // 512, 16, n))


def unpack_weight(words, scales, fmt):
    g, _, n = scales.shape
    words = np.ascontiguousarray(words).reshape(g, 128, n, -1)
    if fmt == "e4m3":
        vals = words.view(ml_dtypes.float8_e4m3fn).astype(np.float64)
    else:
        nib = np.empty((g, 128, n, 4), np.uint8)
        nib[..., 0::2] = words & 0xF
        nib[..., 1::2] = words >> 4
        vals = E2M1[nib]
    vals = vals * np.repeat(np.exp2(scales.astype(np.float64) - 127.0), 8, axis=1)[..., None]
    return vals.transpose(0, 1, 3, 2).reshape(g * 512, n)


def gelu(v):
    return 0.5 * v * (1.0 + np.tanh(np.sqrt(2.0 / np.pi) * (v + 0.044715 * v**3)))


def bf(x):
    return np.asarray(x, np.float32).astype(ml_dtypes.bfloat16)


def planes(Y):
    n, m = Y.shape
    b = f64(bf(Y)).reshape(n // 32, 32, m)
    amax = np.abs(b).max(1)
    byte = np.clip(np.where(amax > 0, np.frexp(amax)[1] - 1 + 127 - 7, 1), 1, 254)
    codes = (b * np.exp2(127.0 - byte)[:, None, :]).reshape(n, m).astype(np.float32).astype(ml_dtypes.float8_e4m3fn).view(np.uint8)
    words = codes.reshape(n // 512, 128, 4, m).transpose(0, 1, 3, 2)
    return np.ascontiguousarray(words), np.ascontiguousarray(byte.astype(np.uint8).reshape(n // 512, 16, m))


K, K2, T, S, T2, H, N = 1024, 512, 2048, 512, 1024, 1024, 1024

def setup_inputs():
    n = np.random.standard_normal
    s, s2, u = mx_kscale(K)[:, None], mx_kscale(K2)[:, None], mx_kscale(H)[:, None]
    tab_words, tab_scales = pack_weight(n((K, T)) * s, "e4m3")
    tab2_words, tab2_scales = pack_weight(n((K2, T)) * s2, "e4m3")
    w2_words, w2_scales = pack_weight(n((K2, H)) / np.sqrt(K2) / s2, "e2m1")
    perm = np.random.permutation(T2)
    return {
        "tab_words": tab_words, "tab_scales": tab_scales,
        "tab2_words": tab2_words, "tab2_scales": tab2_scales,
        "offs": striped(np.random.permutation(T)[:S]),
        "offs2": striped(np.random.permutation(T)[:S]),
        "offs3": striped(perm[:S]), "offs4": striped(perm[S:]),
        "w1": (n((K, H)) / np.sqrt(K) / s * u.T).astype(np.float32),
        "w2_words": w2_words, "w2_scales": w2_scales,
        "gate": np.random.uniform(0.2, 1.8, (H, S)).astype(np.float32),
        "gain": (np.random.uniform(0.5, 1.5, H) * u[:, 0]).astype(np.float32),
        "wg1": np.exp(0.3 * n((128, S))).astype(np.float32),
        "wg2": np.exp(0.3 * n((128, S))).astype(np.float32),
        "mix": np.random.uniform(-0.5, 1.0, (H, T2)).astype(np.float32),
        "w3": (n((H, N)) / np.sqrt(H) / u * np.exp(0.8 * n(N))).astype(np.float32),
    }

def reference(tab_words, tab_scales, tab2_words, tab2_scales, offs, offs2, offs3, offs4,
              w1, w2_words, w2_scales, gate, gain, wg1, wg2, mix, w3):
    v = unpack_weight(tab_words, tab_scales, "e4m3")[:, unstriped(offs)]
    v2 = unpack_weight(tab2_words, tab2_scales, "e4m3")[:, unstriped(offs2)]
    h1 = f64(gate) * (mxq(f64(w1), 0, "e4m3").T @ v)
    b = unpack_weight(w2_words, w2_scales, "e2m1").T @ v2
    h2 = f64(gain)[:, None] * np.log1p(np.exp(b))
    page = np.zeros((H, T2))
    page[:, unstriped(offs3)] = np.tile(f64(wg1), (H // 128, 1)) * h1
    page[:, unstriped(offs4)] = np.tile(f64(wg2), (H // 128, 1)) * h2
    z = page + f64(mix) * page
    y = mxq(f64(w3), 0, "e4m3").T @ mxq(z, 0, "e4m3")
    words, scales = planes(y)
    return y, words, scales

@@ -1,0 +1,305 @@
+from contextlib import ExitStack
+
+import concourse.mybir as mybir
+from concourse.masks import make_identity
+
+K, K2, T, S, T2, H, N = 1024, 512, 2048, 512, 1024, 1024, 1024
+FLOPS = 2 * K * H * S + 2 * K2 * H * S + 2 * H * N * T2
+
+F32 = mybir.dt.float32
+BF16 = mybir.dt.bfloat16
+I32 = mybir.dt.int32
+U32 = mybir.dt.uint32
+U16 = mybir.dt.uint16
+U8 = mybir.dt.uint8
+E4M3 = mybir.dt.float8_e4m3fn_x4
+E2M1 = mybir.dt.float4_e2m1fn_x4
+ALU = mybir.AluOpType
+ACT = mybir.ActivationFunctionType
+
+P = 128
+PACK = 4
+GROUP = P * PACK
+BANK = 512
+
+
+def tile_list_divertor_tile_weave_kernel(
+    tc, tab_words, tab_scales, tab2_words, tab2_scales, offs, offs2, offs3, offs4,
+    w1, w2_words, w2_scales, gate, gain, wg1, wg2, mix, w3, out_0, out_1, out_2,
+):
+    nc = tc.nc
+    with ExitStack() as ctx:
+        lists = ctx.enter_context(tc.tile_pool(name="lists", bufs=1))
+        sb = ctx.enter_context(tc.tile_pool(name="sb", bufs=1))
+        psum = ctx.enter_context(tc.psum_pool(name="psum", bufs=1))
+
+        def tile(name, shape, dtype, tag=None, bufs=1):
+            return sb.tile(shape, dtype, name=name, tag=tag or name, bufs=bufs, align_bytes=64)
+
+        def bank(name, i):
+            return psum.tile([P, BANK], F32, name=name, tag="bank%d" % i)
+
+        def load_list(name, src):
+            lst = lists.tile([P, S // 16], U16, name=name)
+            nc.sync.dma_start(lst[:], src)
+            return lst
+
+        def load_words(name, src):
+            words = tile(name, [P, T], I32)
+            nc.sync.dma_start(words[:], src.rearrange("p t i -> p (t i)").bitcast(I32))
+            return words
+
+        def zeroed_plane(name, width):
+            plane = tile(name, [P, width], U8)
+            nc.vector.memset(plane[:].bitcast(I32), 0)
+            return plane
+
+        def load_plane(queue, plane, src):
+            passes = src.shape[0]
+            for q in range(4):
+                queue.dma_start(
+                    plane[32 * q : 32 * q + 4 * passes, :].bitcast(I32),
+                    src[:, 4 * q : 4 * q + 4, :].bitcast(I32),
+                )
+
+        def load_weight(name, w, a, g, tag, bufs=1):
+            raw = tile(name, [P, PACK, GROUP], F32, tag, bufs)
+            rows = w[GROUP * a : GROUP * (a + 1), GROUP * g : GROUP * (g + 1)]
+            nc.sync.dma_start(raw[:], rows.rearrange("(p j) c -> p j c", j=PACK))
+            return raw
+
+        def round_weight(name, raw):
+            rounded = tile(name, [P, PACK * GROUP], BF16, "bf", 3)
+            nc.scalar.copy(
+                rounded[:].rearrange("p (t m j) -> p m j t", t=PACK, j=PACK),
+                raw[:].rearrange("p j (m t) -> p m j t", t=PACK),
+            )
+            return rounded
+
+        def quantise(name, rounded):
+            codes = tile(name + "_codes", [P, BANK], U32)
+            scales = tile(name + "_scales", [P, BANK], U8)
+            nc.vector.quantize_mx(out=codes[:].bitcast(E4M3), scales=scales[:], in_=rounded)
+            return codes, scales
+
+        def gather(name, dtype, window, lst):
+            picked = tile(name, [P, S], dtype)
+            nc.vector.tensor_copy(picked[:], window[:].bitcast(dtype).indirect(lst[:]))
+            return picked
+
+        def load_wg(name, wg, t0, t1):
+            dealt = tile(name, [P, t1 - t0, S], F32)
+            rows = wg.rearrange("(q t) j -> q t j", t=PACK)[:, t0:t1, :]
+            for q in range(4):
+                nc.sync.dma_start(dealt[32 * q : 32 * q + 32, :, :], rows)
+            return dealt
+
+        gate_rows = gate.rearrange("(g p t) j -> g p t j", g=2, t=PACK)
+        mix_rows = mix.rearrange("(g p t) c -> g p t c", g=2, t=PACK)
+        out_rows = out_0.rearrange("(g p t) c -> g p t c", g=2, t=PACK)
+
+        tab_plane = zeroed_plane("tab_plane", T)
+        tab2_plane = zeroed_plane("tab2_plane", T)
+        w2_plane = zeroed_plane("w2_plane", H)
+        load_plane(nc.scalar, tab_plane, tab_scales)
+        idx = load_list("idx", offs)
+        w1_raw = {}
+        w1_raw[0, 0] = load_weight("w1_00", w1, 0, 0, "slot0")
+        w1_raw[1, 0] = load_weight("w1_10", w1, 1, 0, "slot1")
+        tab = [load_words("tab%d" % a, tab_words[a]) for a in range(2)]
+        idx3 = load_list("idx3", offs3)
+        gates = [tile("gate%d" % g, [P, PACK, S], F32, "gz%d" % g) for g in range(2)]
+        nc.sync.dma_start(gates[0][:, 0, :], gate_rows[0][:, 0, :])
+        wg1_first = load_wg("wg1_first", wg1, 0, 1)
+        nc.sync.dma_start(gates[0][:, 1, :], gate_rows[0][:, 1, :])
+        wg1_rest = load_wg("wg1_rest", wg1, 1, 4)
+        nc.sync.dma_start(gates[0][:, 2:4, :], gate_rows[0][:, 2:4, :])
+        w1_raw[0, 1] = load_weight("w1_01", w1, 0, 1, "slot2")
+        w1_raw[1, 1] = load_weight("w1_11", w1, 1, 1, "slot3")
+        idx2 = load_list("idx2", offs2)
+        load_plane(nc.sync, tab2_plane, tab2_scales)
+        load_plane(nc.sync, w2_plane, w2_scales)
+        tab2 = load_words("tab2", tab2_words[0])
+        w2_codes = tile("w2_codes", [P, 2 * H], U8)
+        nc.sync.dma_start(w2_codes[:].bitcast(I32), w2_words[0].bitcast(I32))
+        nc.sync.dma_start(gates[1][:], gate_rows[1])
+        gains = tile("gains", [P, 2, PACK], F32)
+        nc.sync.dma_start(gains[:], gain.rearrange("(g p t) -> p g t", g=2, t=PACK))
+        idx4 = load_list("idx4", offs4)
+        wg2_all = load_wg("wg2_all", wg2, 0, 4)
+        ident = tile("ident", [P, P], F32)
+        make_identity(nc, ident[:])
+
+        def wg1_of(t):
+            return wg1_first[:, 0, :] if t == 0 else wg1_rest[:, t - 1, :]
+
+        w1_q = {}
+        for a in range(2):
+            w1_q[a, 0] = quantise("w1q%d0" % a, round_weight("w1b%d0" % a, w1_raw[a, 0])[:])
+        v0 = gather("v0", U32, tab[0], idx)
+        v_scales = gather("v_scales", U8, tab_plane, idx)
+        v = [v0, gather("v1", U32, tab[1], idx)]
+        pages = [tile("page%d" % s, [P, T2], F32) for s in range(8)]
+
+        def gated(s):
+            g, t = divmod(s, PACK)
+            acc = bank("h1_%d" % s, t)
+            cols = slice(P * t, P * (t + 1))
+            for a in range(2):
+                codes, scales = w1_q[a, g]
+                nc.tensor.matmul_mx(
+                    acc[:], lhsT=codes[:, cols].bitcast(E4M3), lhsT_scale=scales[:, cols],
+                    rhs=v[a][:].bitcast(E4M3), rhs_scale=v_scales[4 * a : P, :],
+                    start=(a == 0), stop=(a == 1),
+                )
+            h1 = tile("h1s_%d" % s, [P, S], F32, "h1", 3)
+            nc.vector.tensor_tensor(h1[:], acc[:], gates[g][:, t, :], ALU.mult)
+            return h1
+
+        def weave(s, lst, values, weights):
+            nc.vector.tensor_tensor(pages[s][:].indirect(lst[:]), values[:], weights, ALU.mult)
+
+        h1 = {0: gated(0)}
+        for s in range(8):
+            if s == 3:
+                for a in range(2):
+                    w1_q[a, 1] = quantise("w1q%d1" % a, round_weight("w1b%d1" % a, w1_raw[a, 1])[:])
+                v2_scales = gather("v2_scales", U8, tab2_plane, idx2)
+                v2 = gather("v2", U32, tab2, idx2)
+            if s + 1 < 8:
+                h1[s + 1] = gated(s + 1)
+            weave(s, idx3, h1[s], wg1_of(s % PACK))
+
+        mixes = []
+        for k in range(4):
+            g, half = divmod(k, 2)
+            m = tile("mix%d" % k, [P, 2, T2], F32, "slot%d" % k)
+            nc.sync.dma_start(m[:], mix_rows[g][:, 2 * half : 2 * half + 2, :])
+            mixes.append(m)
+
+        def softplus_terms(g):
+            tail = tile("tail%d" % g, [P, 4, PACK, P], F32, "spa")
+            ramp = tile("ramp%d" % g, [P, 4, PACK, P], F32, "spb")
+            for jc in range(4):
+                acc = bank("b_%d_%d" % (g, jc), 4 + jc)
+                cols = slice(P * jc, P * (jc + 1))
+                nc.tensor.matmul_mx(
+                    acc[:], lhsT=v2[:, cols].bitcast(E4M3), lhsT_scale=v2_scales[:, cols],
+                    rhs=w2_codes[:, 2 * GROUP * g : 2 * GROUP * (g + 1)].bitcast(E2M1),
+                    rhs_scale=w2_plane[:, GROUP * g : GROUP * (g + 1)],
+                    start=True, stop=True,
+                )
+                dealt = acc[:].rearrange("p (m t) -> p t m", t=PACK)
+                nc.scalar.activation(tail[:, jc, :, :], dealt, ACT.Abs)
+                nc.scalar.activation(ramp[:, jc, :, :], dealt, ACT.Relu)
+            flat = tail[:].rearrange("p a t m -> p (a t m)")
+            nc.scalar.activation(flat, flat, ACT.Exp, scale=-1.0)
+            nc.scalar.activation(flat, flat, ACT.Ln, bias=1.0)
+            sums = []
+            for t in range(PACK):
+                acc = bank("sp_%d_%d" % (g, t), t)
+                for jc in range(4):
+                    cols = slice(P * jc, P * (jc + 1))
+                    nc.tensor.matmul(acc[:, cols], ramp[:, jc, t, :], ident[:], start=True, stop=False, is_transpose=True)
+                    nc.tensor.matmul(acc[:, cols], tail[:, jc, t, :], ident[:], start=False, stop=True, is_transpose=True)
+                sums.append(acc)
+            return sums
+
+        def gained(s, acc, tag, bufs):
+            g, t = divmod(s, PACK)
+            h2 = tile("h2_%d" % s, [P, S], F32, tag, bufs)
+            nc.scalar.activation(h2[:], acc[:], ACT.Copy, scale=gains[:, g, t : t + 1])
+            return h2
+
+        z_rows = [tile("zrows%d" % g, [P, PACK, T2], BF16, "gz%d" % g) for g in range(2)]
+
+        def adjust(s, cols):
+            g, t = divmod(s, PACK)
+            nc.vector.scalar_tensor_tensor(
+                z_rows[g][:, t, cols], mixes[s // 2][:, s % 2, cols], 1.0, pages[s][:, cols], ALU.add, ALU.mult
+            )
+
+        def interleave(copy, dst, src):
+            copy(dst.rearrange("p (c i t) -> p c t i", i=4, t=PACK), src.rearrange("p t (c i) -> p c t i", i=4))
+
+        everything = slice(0, T2)
+        chunks = [slice(BANK * c, BANK * (c + 1)) for c in range(2)]
+        h2 = {}
+        sums = softplus_terms(0)
+        for t in range(PACK):
+            h2[t] = gained(t, sums[t], "h2", 4)
+        sums = softplus_terms(1)
+        for t in range(2):
+            h2[4 + t] = gained(4 + t, sums[t], "h2", 4)
+        for s in range(6):
+            weave(s, idx4, h2[s], wg2_all[:, s % PACK, :])
+            if s > 0:
+                adjust(s - 1, everything)
+
+        w3_q = {}
+        for a in range(2):
+            for g in range(2):
+                raw = load_weight("w3_%d%d" % (a, g), w3, a, g, "w3raw", 2)
+                w3_q[a, g] = quantise("w3q%d%d" % (a, g), round_weight("w3b%d%d" % (a, g), raw)[:])
+
+        z_q = {}
+        for c in range(2):
+            zi = tile("zi0%d" % c, [P, PACK * BANK], BF16, ("spa", "spb")[c])
+            interleave(nc.scalar.copy, zi[:], z_rows[0][:, :, chunks[c]])
+            z_q[0, c] = quantise("zq0%d" % c, zi[:])
+        h2[6] = gained(6, sums[2], "spa", 1)
+        h2[7] = gained(7, sums[3], "spb", 1)
+
+        def product(acc, a, n, c):
+            g, t = divmod(n, PACK)
+            cols = slice(P * t, P * (t + 1))
+            nc.tensor.matmul_mx(
+                acc[:], lhsT=w3_q[a, g][0][:, cols].bitcast(E4M3), lhsT_scale=w3_q[a, g][1][:, cols],
+                rhs=z_q[a, c][0][:].bitcast(E4M3), rhs_scale=z_q[a, c][1][:],
+                start=(a == 0), stop=(a == 1),
+            )
+
+        early = [bank("y_0_%d" % n, n) for n in range(8)]
+        for n in range(8):
+            product(early[n], 0, n, 0)
+
+        weave(6, idx4, h2[6], wg2_all[:, 2, :])
+        adjust(5, everything)
+        adjust(6, everything)
+        weave(7, idx4, h2[7], wg2_all[:, 3, :])
+        for c in range(2):
+            adjust(7, chunks[c])
+            zi = tile("zi1%d" % c, [P, PACK * BANK], BF16, "bf", 3)
+            half = BANK // 2
+            lo = BANK * c
+            interleave(nc.vector.tensor_copy, zi[:, 0 : PACK * half], z_rows[1][:, :, lo : lo + half])
+            interleave(nc.scalar.copy if c == 0 else nc.vector.tensor_copy,
+                       zi[:, PACK * half : PACK * BANK], z_rows[1][:, :, lo + half : lo + BANK])
+            z_q[1, c] = quantise("zq1%d" % c, zi[:])
+
+        y_scales = [tile("y_scales%d" % g, [P, T2], U8) for g in range(2)]
+        for c in range(2):
+            for g in range(2):
+                y = tile("y%d%d" % (c, g), [P, PACK, BANK], F32, "slot%d" % (2 * c + g))
+                for t in range(PACK):
+                    n = PACK * g + t
+                    if c == 0:
+                        acc = early[n]
+                    else:
+                        acc = bank("y_1_%d" % n, n)
+                        product(acc, 0, n, c)
+                    product(acc, 1, n, c)
+                    nc.scalar.copy(y[:, t, :], acc[:])
+                    nc.sync.dma_start(out_rows[g][:, t, chunks[c]], y[:, t, :])
+                yb = tile("yb%d%d" % (c, g), [P, PACK * BANK], BF16, "bf", 3)
+                interleave(nc.vector.tensor_copy, yb[:], y[:])
+                codes = tile("y_codes%d%d" % (c, g), [P, BANK], U32)
+                nc.vector.quantize_mx(out=codes[:].bitcast(E4M3), scales=y_scales[g][:, chunks[c]], in_=yb[:])
+                words = out_1[g].rearrange("p m t -> p (m t)").bitcast(I32)
+                nc.sync.dma_start(words[:, chunks[c]], codes[:].bitcast(I32))
+                if c == 1:
+                    for q in range(4):
+                        nc.sync.dma_start(
+                            out_2[g][4 * q : 4 * q + 4, :].bitcast(I32),
+                            y_scales[g][32 * q : 32 * q + 4, :].bitcast(I32),
+                        )

@@ -62,25 +62,24 @@ def tile_list_divertor_tile_weave_kernel(
                     src[:, 4 * q : 4 * q + 4, :].bitcast(I32),
                 )
 
-        def load_weight(name, w, a, g, tag, bufs=1):
-            raw = tile(name, [P, PACK, GROUP], F32, tag, bufs)
+        def load_weight(raw, w, a, g):
             rows = w[GROUP * a : GROUP * (a + 1), GROUP * g : GROUP * (g + 1)]
-            nc.sync.dma_start(raw[:], rows.rearrange("(p j) c -> p j c", j=PACK))
+            nc.sync.dma_start(raw, rows.rearrange("(p j) c -> p j c", j=PACK))
             return raw
 
-        def round_weight(name, raw):
-            rounded = tile(name, [P, PACK * GROUP], BF16, "bf", 3)
-            nc.scalar.copy(
-                rounded[:].rearrange("p (t m j) -> p m j t", t=PACK, j=PACK),
-                raw[:].rearrange("p j (m t) -> p m j t", t=PACK),
+        def round_weight(rounded, raw):
+            nc.scalar.activation(
+                rounded.rearrange("p (t m j) -> p m j t", t=PACK, j=PACK),
+                raw.rearrange("p j (m t) -> p m j t", t=PACK),
+                ACT.Copy,
             )
-            return rounded
 
         def quantise(name, rounded):
-            codes = tile(name + "_codes", [P, BANK], U32)
-            scales = tile(name + "_scales", [P, BANK], U8)
+            width = rounded.shape[1] // PACK
+            codes = tile(name + "_codes", [P, width], U32)
+            scales = tile(name + "_scales", [P, width], U8)
             nc.vector.quantize_mx(out=codes[:].bitcast(E4M3), scales=scales[:], in_=rounded)
-            return codes, scales
+            return [(codes[:, c : c + BANK], scales[:, c : c + BANK]) for c in range(0, width, BANK)]
 
         def gather(name, dtype, window, lst):
             picked = tile(name, [P, S], dtype)
@@ -101,28 +100,34 @@ def tile_list_divertor_tile_weave_kernel(
         tab_plane = zeroed_plane("tab_plane", T)
         tab2_plane = zeroed_plane("tab2_plane", T)
         w2_plane = zeroed_plane("w2_plane", H)
-        load_plane(nc.scalar, tab_plane, tab_scales)
+        staged = tile("staged_scales", [P, T], U8, "bfB")
+        load_plane(nc.scalar, staged, tab_scales)
+        for q in range(4):
+            rows = slice(32 * q, 32 * q + 8)
+            nc.vector.tensor_copy(tab_plane[rows, :].bitcast(I32), staged[rows, :].bitcast(I32))
         idx = load_list("idx", offs)
         w1_raw = {}
-        w1_raw[0, 0] = load_weight("w1_00", w1, 0, 0, "slot0")
-        w1_raw[1, 0] = load_weight("w1_10", w1, 1, 0, "slot1")
+        for a in range(2):
+            w1_raw[a, 0] = load_weight(tile("w1_%d0" % a, [P, PACK, GROUP], F32, "slot%d" % a)[:], w1, a, 0)
         tab = [load_words("tab%d" % a, tab_words[a]) for a in range(2)]
         idx3 = load_list("idx3", offs3)
-        gates = [tile("gate%d" % g, [P, PACK, S], F32, "gz%d" % g) for g in range(2)]
+        both_gates = tile("gates", [P, 2, PACK, S], F32, "gz")
+        gates = [both_gates[:, g] for g in range(2)]
         nc.sync.dma_start(gates[0][:, 0, :], gate_rows[0][:, 0, :])
         wg1_first = load_wg("wg1_first", wg1, 0, 1)
         nc.sync.dma_start(gates[0][:, 1, :], gate_rows[0][:, 1, :])
         wg1_rest = load_wg("wg1_rest", wg1, 1, 4)
-        nc.sync.dma_start(gates[0][:, 2:4, :], gate_rows[0][:, 2:4, :])
-        w1_raw[0, 1] = load_weight("w1_01", w1, 0, 1, "slot2")
-        w1_raw[1, 1] = load_weight("w1_11", w1, 1, 1, "slot3")
         idx2 = load_list("idx2", offs2)
         load_plane(nc.sync, tab2_plane, tab2_scales)
         load_plane(nc.sync, w2_plane, w2_scales)
         tab2 = load_words("tab2", tab2_words[0])
         w2_codes = tile("w2_codes", [P, 2 * H], U8)
         nc.sync.dma_start(w2_codes[:].bitcast(I32), w2_words[0].bitcast(I32))
-        nc.sync.dma_start(gates[1][:], gate_rows[1])
+        nc.sync.dma_start(gates[0][:, 2:4, :], gate_rows[0][:, 2:4, :])
+        w1_late = tile("w1_late", [P, 2, PACK, GROUP], F32, "slot2")
+        for a in range(2):
+            w1_raw[a, 1] = load_weight(w1_late[:, a], w1, a, 1)
+        nc.sync.dma_start(gates[1], gate_rows[1])
         gains = tile("gains", [P, 2, PACK], F32)
         nc.sync.dma_start(gains[:], gain.rearrange("(g p t) -> p g t", g=2, t=PACK))
         idx4 = load_list("idx4", offs4)
@@ -133,9 +138,13 @@ def tile_list_divertor_tile_weave_kernel(
         def wg1_of(t):
             return wg1_first[:, 0, :] if t == 0 else wg1_rest[:, t - 1, :]
 
+        WIDE = PACK * GROUP
         w1_q = {}
+        rounded = tile("w1b0", [P, 2 * WIDE], BF16, "bfA")
         for a in range(2):
-            w1_q[a, 0] = quantise("w1q%d0" % a, round_weight("w1b%d0" % a, w1_raw[a, 0])[:])
+            part = rounded[:, WIDE * a : WIDE * (a + 1)]
+            round_weight(part, w1_raw[a, 0])
+            w1_q[a, 0] = quantise("w1q%d0" % a, part)[0]
         v0 = gather("v0", U32, tab[0], idx)
         v_scales = gather("v_scales", U8, tab_plane, idx)
         v = [v0, gather("v1", U32, tab[1], idx)]
@@ -143,6 +152,8 @@ def tile_list_divertor_tile_weave_kernel(
 
         def gated(s):
             g, t = divmod(s, PACK)
+            engine = nc.vector if s == 0 else nc.gpsimd
+            engine.tensor_tensor(gates[g][:, t, :], gates[g][:, t, :], wg1_of(t), ALU.mult)
             acc = bank("h1_%d" % s, t)
             cols = slice(P * t, P * (t + 1))
             for a in range(2):
@@ -152,34 +163,42 @@ def tile_list_divertor_tile_weave_kernel(
                     rhs=v[a][:].bitcast(E4M3), rhs_scale=v_scales[4 * a : P, :],
                     start=(a == 0), stop=(a == 1),
                 )
-            h1 = tile("h1s_%d" % s, [P, S], F32, "h1", 3)
+            if s == 3:
+                h1 = tile("h1s_%d" % s, [P, S], F32, "bfB")
+            else:
+                h1 = tile("h1s_%d" % s, [P, S], F32, "h1", 3)
             nc.vector.tensor_tensor(h1[:], acc[:], gates[g][:, t, :], ALU.mult)
             return h1
 
-        def weave(s, lst, values, weights):
-            nc.vector.tensor_tensor(pages[s][:].indirect(lst[:]), values[:], weights, ALU.mult)
+        def weave(s, lst, values):
+            nc.vector.tensor_copy(pages[s][:].indirect(lst[:]), values)
 
         h1 = {0: gated(0)}
         for s in range(8):
-            if s == 3:
-                for a in range(2):
-                    w1_q[a, 1] = quantise("w1q%d1" % a, round_weight("w1b%d1" % a, w1_raw[a, 1])[:])
+            if s == 1:
                 v2_scales = gather("v2_scales", U8, tab2_plane, idx2)
                 v2 = gather("v2", U32, tab2, idx2)
+            if s == 2:
+                rounded = tile("w1b1", [P, 2 * WIDE], BF16, "bfB")
+                for a in range(2):
+                    round_weight(rounded[:, WIDE * a : WIDE * (a + 1)], w1_raw[a, 1])
+                w1_q[0, 1], w1_q[1, 1] = quantise("w1q1", rounded[:])
             if s + 1 < 8:
                 h1[s + 1] = gated(s + 1)
-            weave(s, idx3, h1[s], wg1_of(s % PACK))
+            weave(s, idx3, h1[s][:])
 
         mixes = []
-        for k in range(4):
-            g, half = divmod(k, 2)
-            m = tile("mix%d" % k, [P, 2, T2], F32, "slot%d" % k)
-            nc.sync.dma_start(m[:], mix_rows[g][:, 2 * half : 2 * half + 2, :])
-            mixes.append(m)
+        for half in range(2):
+            m = tile("mix%d" % half, [P, 2, T2], F32, "slot%d" % half)
+            nc.sync.dma_start(m[:], mix_rows[0][:, 2 * half : 2 * half + 2, :])
+            for t in range(2):
+                nc.gpsimd.tensor_scalar(m[:, t, :], m[:, t, :], 1.0, 1.0, ALU.add, ALU.mult)
+                mixes.append(m[:, t, :])
 
-        def softplus_terms(g):
-            tail = tile("tail%d" % g, [P, 4, PACK, P], F32, "spa")
-            ramp = tile("ramp%d" % g, [P, 4, PACK, P], F32, "spb")
+        terms = tile("terms0", [P, 2, 4, PACK, P], F32, "slot2")
+        tails = [terms[:, 0], tile("tail1", [P, 4, PACK, P], F32, "spa")[:]]
+        ramps = [terms[:, 1], tile("ramp1", [P, 4, PACK, P], F32, "spb")[:]]
+        for g in range(2):
             for jc in range(4):
                 acc = bank("b_%d_%d" % (g, jc), 4 + jc)
                 cols = slice(P * jc, P * (jc + 1))
@@ -190,72 +209,80 @@ def tile_list_divertor_tile_weave_kernel(
                     start=True, stop=True,
                 )
                 dealt = acc[:].rearrange("p (m t) -> p t m", t=PACK)
-                nc.scalar.activation(tail[:, jc, :, :], dealt, ACT.Abs)
-                nc.scalar.activation(ramp[:, jc, :, :], dealt, ACT.Relu)
-            flat = tail[:].rearrange("p a t m -> p (a t m)")
-            nc.scalar.activation(flat, flat, ACT.Exp, scale=-1.0)
-            nc.scalar.activation(flat, flat, ACT.Ln, bias=1.0)
-            sums = []
-            for t in range(PACK):
-                acc = bank("sp_%d_%d" % (g, t), t)
-                for jc in range(4):
-                    cols = slice(P * jc, P * (jc + 1))
-                    nc.tensor.matmul(acc[:, cols], ramp[:, jc, t, :], ident[:], start=True, stop=False, is_transpose=True)
-                    nc.tensor.matmul(acc[:, cols], tail[:, jc, t, :], ident[:], start=False, stop=True, is_transpose=True)
-                sums.append(acc)
-            return sums
+                nc.scalar.activation(tails[g][:, jc, :, :], dealt, ACT.Abs)
+                nc.scalar.activation(ramps[g][:, jc, :, :], dealt, ACT.Relu)
+        flats = [tails[g].rearrange("p a t m -> p (a t m)") for g in range(2)]
+        for g in range(2):
+            nc.scalar.activation(flats[g], flats[g], ACT.Exp, scale=-1.0)
+        for g in range(2):
+            nc.scalar.activation(flats[g], flats[g], ACT.Ln, bias=1.0)
 
-        def gained(s, acc, tag, bufs):
+        def softplus(s):
             g, t = divmod(s, PACK)
-            h2 = tile("h2_%d" % s, [P, S], F32, tag, bufs)
-            nc.scalar.activation(h2[:], acc[:], ACT.Copy, scale=gains[:, g, t : t + 1])
+            acc = bank("sp_%d" % s, 4 + t)
+            for jc in range(4):
+                cols = slice(P * jc, P * (jc + 1))
+                nc.tensor.matmul(acc[:, cols], ramps[g][:, jc, t, :], ident[:], start=True, stop=False, is_transpose=True)
+                nc.tensor.matmul(acc[:, cols], tails[g][:, jc, t, :], ident[:], start=False, stop=True, is_transpose=True)
+            return acc
+
+        def weighted(s, gained, h2):
+            g, t = divmod(s, PACK)
+            nc.scalar.activation(gained, softplus(s)[:], ACT.Copy, scale=gains[:, g, t : t + 1])
+            nc.gpsimd.tensor_tensor(h2, gained, wg2_all[:, t, :], ALU.mult)
             return h2
-
-        z_rows = [tile("zrows%d" % g, [P, PACK, T2], BF16, "gz%d" % g) for g in range(2)]
-
-        def adjust(s, cols):
-            g, t = divmod(s, PACK)
-            nc.vector.scalar_tensor_tensor(
-                z_rows[g][:, t, cols], mixes[s // 2][:, s % 2, cols], 1.0, pages[s][:, cols], ALU.add, ALU.mult
-            )
 
         def interleave(copy, dst, src):
             copy(dst.rearrange("p (c i t) -> p c t i", i=4, t=PACK), src.rearrange("p t (c i) -> p c t i", i=4))
 
-        everything = slice(0, T2)
         chunks = [slice(BANK * c, BANK * (c + 1)) for c in range(2)]
         h2 = {}
-        sums = softplus_terms(0)
         for t in range(PACK):
-            h2[t] = gained(t, sums[t], "h2", 4)
-        sums = softplus_terms(1)
-        for t in range(2):
-            h2[4 + t] = gained(4 + t, sums[t], "h2", 4)
-        for s in range(6):
-            weave(s, idx4, h2[s], wg2_all[:, s % PACK, :])
-            if s > 0:
-                adjust(s - 1, everything)
+            both = tile("h2_%d" % t, [P, S], F32)
+            h2[t] = weighted(t, both[:], both[:])
+        gained = tile("gained", [P, 3, S], F32, "gz")
+        h2_late = tile("h2_late", [P, 3, S], F32, "wg1_rest")
+        for t in range(3):
+            h2[4 + t] = weighted(4 + t, gained[:, t, :], h2_late[:, t, :])
+        last_sum = softplus(7)
+        m = tile("mix2", [P, PACK, T2], F32, "slot2")
+        for half in range(2):
+            nc.sync.dma_start(m[:, 2 * half : 2 * half + 2, :], mix_rows[1][:, 2 * half : 2 * half + 2, :])
+        for t in range(PACK):
+            if t < 3:
+                nc.scalar.activation(m[:, t, :], m[:, t, :], ACT.Identity, bias=1.0)
+            mixes.append(m[:, t, :])
+
+        both_rows = tile("z_rows", [P, 2, PACK, T2], BF16, "gz")
+        z_rows = [both_rows[:, g] for g in range(2)]
+        for s in range(7):
+            g, t = divmod(s, PACK)
+            weave(s, idx4, h2[s])
+            for cols in chunks:
+                nc.gpsimd.tensor_tensor(z_rows[g][:, t, cols], mixes[s][:, cols], pages[s][:, cols], ALU.mult)
 
         w3_q = {}
         for a in range(2):
+            rounded = tile("w3b%d" % a, [P, 2 * WIDE], BF16, ("spb", "bfA")[a])
             for g in range(2):
-                raw = load_weight("w3_%d%d" % (a, g), w3, a, g, "w3raw", 2)
-                w3_q[a, g] = quantise("w3q%d%d" % (a, g), round_weight("w3b%d%d" % (a, g), raw)[:])
+                raw = load_weight(tile("w3_%d%d" % (a, g), [P, PACK, GROUP], F32, "w3raw", 2)[:], w3, a, g)
+                round_weight(rounded[:, WIDE * g : WIDE * (g + 1)], raw)
+            w3_q[a, 0], w3_q[a, 1] = quantise("w3q%d" % a, rounded[:])
 
         z_q = {}
+        zi = tile("zi0", [P, 2 * WIDE], BF16, "spa")
         for c in range(2):
-            zi = tile("zi0%d" % c, [P, PACK * BANK], BF16, ("spa", "spb")[c])
-            interleave(nc.scalar.copy, zi[:], z_rows[0][:, :, chunks[c]])
-            z_q[0, c] = quantise("zq0%d" % c, zi[:])
-        h2[6] = gained(6, sums[2], "spa", 1)
-        h2[7] = gained(7, sums[3], "spb", 1)
+            interleave(nc.scalar.copy, zi[:, WIDE * c : WIDE * (c + 1)], z_rows[0][:, :, chunks[c]])
+        z_q[0, 0], z_q[0, 1] = quantise("zq0", zi[:])
+        last = tile("h2_7", [P, S], F32, "spa")
+        nc.vector.scalar_tensor_tensor(last[:], last_sum[:], gains[:, 1, 3:4], wg2_all[:, 3, :], ALU.mult, ALU.mult)
 
         def product(acc, a, n, c):
             g, t = divmod(n, PACK)
             cols = slice(P * t, P * (t + 1))
             nc.tensor.matmul_mx(
                 acc[:], lhsT=w3_q[a, g][0][:, cols].bitcast(E4M3), lhsT_scale=w3_q[a, g][1][:, cols],
-                rhs=z_q[a, c][0][:].bitcast(E4M3), rhs_scale=z_q[a, c][1][:],
+                rhs=z_q[a, c][0].bitcast(E4M3), rhs_scale=z_q[a, c][1],
                 start=(a == 0), stop=(a == 1),
             )
 
@@ -263,24 +290,26 @@ def tile_list_divertor_tile_weave_kernel(
         for n in range(8):
             product(early[n], 0, n, 0)
 
-        weave(6, idx4, h2[6], wg2_all[:, 2, :])
-        adjust(5, everything)
-        adjust(6, everything)
-        weave(7, idx4, h2[7], wg2_all[:, 3, :])
+        weave(7, idx4, last[:])
+        zi = tile("zi1", [P, 2 * WIDE], BF16, "bfA")
         for c in range(2):
-            adjust(7, chunks[c])
-            zi = tile("zi1%d" % c, [P, PACK * BANK], BF16, "bf", 3)
+            cols = chunks[c]
+            nc.vector.scalar_tensor_tensor(
+                z_rows[1][:, 3, cols], mixes[7][:, cols], 1.0, pages[7][:, cols], ALU.add, ALU.mult
+            )
             half = BANK // 2
             lo = BANK * c
-            interleave(nc.vector.tensor_copy, zi[:, 0 : PACK * half], z_rows[1][:, :, lo : lo + half])
+            part = zi[:, WIDE * c : WIDE * (c + 1)]
+            interleave(nc.vector.tensor_copy, part[:, 0 : PACK * half], z_rows[1][:, :, lo : lo + half])
             interleave(nc.scalar.copy if c == 0 else nc.vector.tensor_copy,
-                       zi[:, PACK * half : PACK * BANK], z_rows[1][:, :, lo + half : lo + BANK])
-            z_q[1, c] = quantise("zq1%d" % c, zi[:])
+                       part[:, PACK * half : PACK * BANK], z_rows[1][:, :, lo + half : lo + BANK])
+            z_q[1, c] = quantise("zq1%d" % c, part)[0]
 
         y_scales = [tile("y_scales%d" % g, [P, T2], U8) for g in range(2)]
+        y_late = tile("y_late", [P, 2, PACK, BANK], F32, "slot2")
         for c in range(2):
             for g in range(2):
-                y = tile("y%d%d" % (c, g), [P, PACK, BANK], F32, "slot%d" % (2 * c + g))
+                y = tile("y%d" % g, [P, PACK, BANK], F32, "slot%d" % g)[:] if c == 0 else y_late[:, g]
                 for t in range(PACK):
                     n = PACK * g + t
                     if c == 0:
@@ -291,8 +320,8 @@ def tile_list_divertor_tile_weave_kernel(
                     product(acc, 1, n, c)
                     nc.scalar.copy(y[:, t, :], acc[:])
                     nc.sync.dma_start(out_rows[g][:, t, chunks[c]], y[:, t, :])
-                yb = tile("yb%d%d" % (c, g), [P, PACK * BANK], BF16, "bf", 3)
-                interleave(nc.vector.tensor_copy, yb[:], y[:])
+                yb = tile("yb%d%d" % (c, g), [P, WIDE], BF16, ("bfB", "spb", "spa", "bfB")[2 * c + g])
+                interleave(nc.vector.tensor_copy, yb[:], y)
                 codes = tile("y_codes%d%d" % (c, g), [P, BANK], U32)
                 nc.vector.quantize_mx(out=codes[:].bitcast(E4M3), scales=y_scales[g][:, chunks[c]], in_=yb[:])
                 words = out_1[g].rearrange("p m t -> p (m t)").bitcast(I32)

from contextlib import ExitStack

import concourse.mybir as mybir
from concourse.masks import make_identity

K, K2, T, S, T2, H, N = 1024, 512, 2048, 512, 1024, 1024, 1024
FLOPS = 2 * K * H * S + 2 * K2 * H * S + 2 * H * N * T2

F32 = mybir.dt.float32
BF16 = mybir.dt.bfloat16
I32 = mybir.dt.int32
U32 = mybir.dt.uint32
U16 = mybir.dt.uint16
U8 = mybir.dt.uint8
E4M3 = mybir.dt.float8_e4m3fn_x4
E2M1 = mybir.dt.float4_e2m1fn_x4
ALU = mybir.AluOpType
ACT = mybir.ActivationFunctionType

P = 128
PACK = 4
GROUP = P * PACK
BANK = 512


def tile_list_divertor_tile_weave_kernel(
    tc, tab_words, tab_scales, tab2_words, tab2_scales, offs, offs2, offs3, offs4,
    w1, w2_words, w2_scales, gate, gain, wg1, wg2, mix, w3, out_0, out_1, out_2,
):
    nc = tc.nc
    with ExitStack() as ctx:
        lists = ctx.enter_context(tc.tile_pool(name="lists", bufs=1))
        sb = ctx.enter_context(tc.tile_pool(name="sb", bufs=1))
        psum = ctx.enter_context(tc.psum_pool(name="psum", bufs=1))

        def tile(name, shape, dtype, tag=None, bufs=1):
            return sb.tile(shape, dtype, name=name, tag=tag or name, bufs=bufs, align_bytes=64)

        def bank(name, i):
            return psum.tile([P, BANK], F32, name=name, tag="bank%d" % i)

        def load_list(name, src):
            lst = lists.tile([P, S // 16], U16, name=name)
            nc.sync.dma_start(lst[:], src)
            return lst

        def load_words(name, src):
            words = tile(name, [P, T], I32)
            nc.sync.dma_start(words[:], src.rearrange("p t i -> p (t i)").bitcast(I32))
            return words

        def zeroed_plane(name, width):
            plane = tile(name, [P, width], U8)
            nc.vector.memset(plane[:].bitcast(I32), 0)
            return plane

        def load_plane(queue, plane, src):
            passes = src.shape[0]
            for q in range(4):
                queue.dma_start(
                    plane[32 * q : 32 * q + 4 * passes, :].bitcast(I32),
                    src[:, 4 * q : 4 * q + 4, :].bitcast(I32),
                )

        def load_weight(raw, w, a, g):
            rows = w[GROUP * a : GROUP * (a + 1), GROUP * g : GROUP * (g + 1)]
            nc.sync.dma_start(raw, rows.rearrange("(p j) c -> p j c", j=PACK))
            return raw

        def round_weight(rounded, raw):
            nc.scalar.activation(
                rounded.rearrange("p (t m j) -> p m j t", t=PACK, j=PACK),
                raw.rearrange("p j (m t) -> p m j t", t=PACK),
                ACT.Copy,
            )

        def quantise(name, rounded):
            width = rounded.shape[1] // PACK
            codes = tile(name + "_codes", [P, width], U32)
            scales = tile(name + "_scales", [P, width], U8)
            nc.vector.quantize_mx(out=codes[:].bitcast(E4M3), scales=scales[:], in_=rounded)
            return [(codes[:, c : c + BANK], scales[:, c : c + BANK]) for c in range(0, width, BANK)]

        def gather(name, dtype, window, lst):
            picked = tile(name, [P, S], dtype)
            nc.vector.tensor_copy(picked[:], window[:].bitcast(dtype).indirect(lst[:]))
            return picked

        def load_wg(name, wg, t0, t1):
            dealt = tile(name, [P, t1 - t0, S], F32)
            rows = wg.rearrange("(q t) j -> q t j", t=PACK)[:, t0:t1, :]
            for q in range(4):
                nc.sync.dma_start(dealt[32 * q : 32 * q + 32, :, :], rows)
            return dealt

        gate_rows = gate.rearrange("(g p t) j -> g p t j", g=2, t=PACK)
        mix_rows = mix.rearrange("(g p t) c -> g p t c", g=2, t=PACK)
        out_rows = out_0.rearrange("(g p t) c -> g p t c", g=2, t=PACK)

        tab_plane = zeroed_plane("tab_plane", T)
        tab2_plane = zeroed_plane("tab2_plane", T)
        w2_plane = zeroed_plane("w2_plane", H)
        staged = tile("staged_scales", [P, T], U8, "bfB")
        load_plane(nc.scalar, staged, tab_scales)
        for q in range(4):
            rows = slice(32 * q, 32 * q + 8)
            nc.vector.tensor_copy(tab_plane[rows, :].bitcast(I32), staged[rows, :].bitcast(I32))
        idx = load_list("idx", offs)
        w1_raw = {}
        for a in range(2):
            w1_raw[a, 0] = load_weight(tile("w1_%d0" % a, [P, PACK, GROUP], F32, "slot%d" % a)[:], w1, a, 0)
        tab = [load_words("tab%d" % a, tab_words[a]) for a in range(2)]
        idx3 = load_list("idx3", offs3)
        both_gates = tile("gates", [P, 2, PACK, S], F32, "gz")
        gates = [both_gates[:, g] for g in range(2)]
        nc.sync.dma_start(gates[0][:, 0, :], gate_rows[0][:, 0, :])
        wg1_first = load_wg("wg1_first", wg1, 0, 1)
        nc.sync.dma_start(gates[0][:, 1, :], gate_rows[0][:, 1, :])
        wg1_rest = load_wg("wg1_rest", wg1, 1, 4)
        idx2 = load_list("idx2", offs2)
        load_plane(nc.sync, tab2_plane, tab2_scales)
        load_plane(nc.sync, w2_plane, w2_scales)
        tab2 = load_words("tab2", tab2_words[0])
        w2_codes = tile("w2_codes", [P, 2 * H], U8)
        nc.sync.dma_start(w2_codes[:].bitcast(I32), w2_words[0].bitcast(I32))
        nc.sync.dma_start(gates[0][:, 2:4, :], gate_rows[0][:, 2:4, :])
        w1_late = tile("w1_late", [P, 2, PACK, GROUP], F32, "slot2")
        for a in range(2):
            w1_raw[a, 1] = load_weight(w1_late[:, a], w1, a, 1)
        nc.sync.dma_start(gates[1], gate_rows[1])
        gains = tile("gains", [P, 2, PACK], F32)
        nc.sync.dma_start(gains[:], gain.rearrange("(g p t) -> p g t", g=2, t=PACK))
        idx4 = load_list("idx4", offs4)
        wg2_all = load_wg("wg2_all", wg2, 0, 4)
        ident = tile("ident", [P, P], F32)
        make_identity(nc, ident[:])

        def wg1_of(t):
            return wg1_first[:, 0, :] if t == 0 else wg1_rest[:, t - 1, :]

        WIDE = PACK * GROUP
        w1_q = {}
        rounded = tile("w1b0", [P, 2 * WIDE], BF16, "bfA")
        for a in range(2):
            part = rounded[:, WIDE * a : WIDE * (a + 1)]
            round_weight(part, w1_raw[a, 0])
            w1_q[a, 0] = quantise("w1q%d0" % a, part)[0]
        v0 = gather("v0", U32, tab[0], idx)
        v_scales = gather("v_scales", U8, tab_plane, idx)
        v = [v0, gather("v1", U32, tab[1], idx)]
        pages = [tile("page%d" % s, [P, T2], F32) for s in range(8)]

        def gated(s):
            g, t = divmod(s, PACK)
            engine = nc.vector if s == 0 else nc.gpsimd
            engine.tensor_tensor(gates[g][:, t, :], gates[g][:, t, :], wg1_of(t), ALU.mult)
            acc = bank("h1_%d" % s, t)
            cols = slice(P * t, P * (t + 1))
            for a in range(2):
                codes, scales = w1_q[a, g]
                nc.tensor.matmul_mx(
                    acc[:], lhsT=codes[:, cols].bitcast(E4M3), lhsT_scale=scales[:, cols],
                    rhs=v[a][:].bitcast(E4M3), rhs_scale=v_scales[4 * a : P, :],
                    start=(a == 0), stop=(a == 1),
                )
            if s == 3:
                h1 = tile("h1s_%d" % s, [P, S], F32, "bfB")
            else:
                h1 = tile("h1s_%d" % s, [P, S], F32, "h1", 3)
            nc.vector.tensor_tensor(h1[:], acc[:], gates[g][:, t, :], ALU.mult)
            return h1

        def weave(s, lst, values):
            nc.vector.tensor_copy(pages[s][:].indirect(lst[:]), values)

        h1 = {0: gated(0)}
        for s in range(8):
            if s == 1:
                v2_scales = gather("v2_scales", U8, tab2_plane, idx2)
                v2 = gather("v2", U32, tab2, idx2)
            if s == 2:
                rounded = tile("w1b1", [P, 2 * WIDE], BF16, "bfB")
                for a in range(2):
                    round_weight(rounded[:, WIDE * a : WIDE * (a + 1)], w1_raw[a, 1])
                w1_q[0, 1], w1_q[1, 1] = quantise("w1q1", rounded[:])
            if s + 1 < 8:
                h1[s + 1] = gated(s + 1)
            weave(s, idx3, h1[s][:])

        mixes = []
        for half in range(2):
            m = tile("mix%d" % half, [P, 2, T2], F32, "slot%d" % half)
            nc.sync.dma_start(m[:], mix_rows[0][:, 2 * half : 2 * half + 2, :])
            for t in range(2):
                nc.gpsimd.tensor_scalar(m[:, t, :], m[:, t, :], 1.0, 1.0, ALU.add, ALU.mult)
                mixes.append(m[:, t, :])

        terms = tile("terms0", [P, 2, 4, PACK, P], F32, "slot2")
        tails = [terms[:, 0], tile("tail1", [P, 4, PACK, P], F32, "spa")[:]]
        ramps = [terms[:, 1], tile("ramp1", [P, 4, PACK, P], F32, "spb")[:]]
        for g in range(2):
            for jc in range(4):
                acc = bank("b_%d_%d" % (g, jc), 4 + jc)
                cols = slice(P * jc, P * (jc + 1))
                nc.tensor.matmul_mx(
                    acc[:], lhsT=v2[:, cols].bitcast(E4M3), lhsT_scale=v2_scales[:, cols],
                    rhs=w2_codes[:, 2 * GROUP * g : 2 * GROUP * (g + 1)].bitcast(E2M1),
                    rhs_scale=w2_plane[:, GROUP * g : GROUP * (g + 1)],
                    start=True, stop=True,
                )
                dealt = acc[:].rearrange("p (m t) -> p t m", t=PACK)
                nc.scalar.activation(tails[g][:, jc, :, :], dealt, ACT.Abs)
                nc.scalar.activation(ramps[g][:, jc, :, :], dealt, ACT.Relu)
        flats = [tails[g].rearrange("p a t m -> p (a t m)") for g in range(2)]
        for g in range(2):
            nc.scalar.activation(flats[g], flats[g], ACT.Exp, scale=-1.0)
        for g in range(2):
            nc.scalar.activation(flats[g], flats[g], ACT.Ln, bias=1.0)

        def softplus(s):
            g, t = divmod(s, PACK)
            acc = bank("sp_%d" % s, 4 + t)
            for jc in range(4):
                cols = slice(P * jc, P * (jc + 1))
                nc.tensor.matmul(acc[:, cols], ramps[g][:, jc, t, :], ident[:], start=True, stop=False, is_transpose=True)
                nc.tensor.matmul(acc[:, cols], tails[g][:, jc, t, :], ident[:], start=False, stop=True, is_transpose=True)
            return acc

        def weighted(s, gained, h2):
            g, t = divmod(s, PACK)
            nc.scalar.activation(gained, softplus(s)[:], ACT.Copy, scale=gains[:, g, t : t + 1])
            nc.gpsimd.tensor_tensor(h2, gained, wg2_all[:, t, :], ALU.mult)
            return h2

        def interleave(copy, dst, src):
            copy(dst.rearrange("p (c i t) -> p c t i", i=4, t=PACK), src.rearrange("p t (c i) -> p c t i", i=4))

        chunks = [slice(BANK * c, BANK * (c + 1)) for c in range(2)]
        h2 = {}
        for t in range(PACK):
            both = tile("h2_%d" % t, [P, S], F32)
            h2[t] = weighted(t, both[:], both[:])
        gained = tile("gained", [P, 3, S], F32, "gz")
        h2_late = tile("h2_late", [P, 3, S], F32, "wg1_rest")
        for t in range(3):
            h2[4 + t] = weighted(4 + t, gained[:, t, :], h2_late[:, t, :])
        last_sum = softplus(7)
        m = tile("mix2", [P, PACK, T2], F32, "slot2")
        for half in range(2):
            nc.sync.dma_start(m[:, 2 * half : 2 * half + 2, :], mix_rows[1][:, 2 * half : 2 * half + 2, :])
        for t in range(PACK):
            if t < 3:
                nc.scalar.activation(m[:, t, :], m[:, t, :], ACT.Identity, bias=1.0)
            mixes.append(m[:, t, :])

        both_rows = tile("z_rows", [P, 2, PACK, T2], BF16, "gz")
        z_rows = [both_rows[:, g] for g in range(2)]
        for s in range(7):
            g, t = divmod(s, PACK)
            weave(s, idx4, h2[s])
            for cols in chunks:
                nc.gpsimd.tensor_tensor(z_rows[g][:, t, cols], mixes[s][:, cols], pages[s][:, cols], ALU.mult)

        w3_q = {}
        for a in range(2):
            rounded = tile("w3b%d" % a, [P, 2 * WIDE], BF16, ("spb", "bfA")[a])
            for g in range(2):
                raw = load_weight(tile("w3_%d%d" % (a, g), [P, PACK, GROUP], F32, "w3raw", 2)[:], w3, a, g)
                round_weight(rounded[:, WIDE * g : WIDE * (g + 1)], raw)
            w3_q[a, 0], w3_q[a, 1] = quantise("w3q%d" % a, rounded[:])

        z_q = {}
        zi = tile("zi0", [P, 2 * WIDE], BF16, "spa")
        for c in range(2):
            interleave(nc.scalar.copy, zi[:, WIDE * c : WIDE * (c + 1)], z_rows[0][:, :, chunks[c]])
        z_q[0, 0], z_q[0, 1] = quantise("zq0", zi[:])
        last = tile("h2_7", [P, S], F32, "spa")
        nc.vector.scalar_tensor_tensor(last[:], last_sum[:], gains[:, 1, 3:4], wg2_all[:, 3, :], ALU.mult, ALU.mult)

        def product(acc, a, n, c):
            g, t = divmod(n, PACK)
            cols = slice(P * t, P * (t + 1))
            nc.tensor.matmul_mx(
                acc[:], lhsT=w3_q[a, g][0][:, cols].bitcast(E4M3), lhsT_scale=w3_q[a, g][1][:, cols],
                rhs=z_q[a, c][0].bitcast(E4M3), rhs_scale=z_q[a, c][1],
                start=(a == 0), stop=(a == 1),
            )

        early = [bank("y_0_%d" % n, n) for n in range(8)]
        for n in range(8):
            product(early[n], 0, n, 0)

        weave(7, idx4, last[:])
        zi = tile("zi1", [P, 2 * WIDE], BF16, "bfA")
        for c in range(2):
            cols = chunks[c]
            nc.vector.scalar_tensor_tensor(
                z_rows[1][:, 3, cols], mixes[7][:, cols], 1.0, pages[7][:, cols], ALU.add, ALU.mult
            )
            half = BANK // 2
            lo = BANK * c
            part = zi[:, WIDE * c : WIDE * (c + 1)]
            interleave(nc.vector.tensor_copy, part[:, 0 : PACK * half], z_rows[1][:, :, lo : lo + half])
            interleave(nc.scalar.copy if c == 0 else nc.vector.tensor_copy,
                       part[:, PACK * half : PACK * BANK], z_rows[1][:, :, lo + half : lo + BANK])
            z_q[1, c] = quantise("zq1%d" % c, part)[0]

        y_scales = [tile("y_scales%d" % g, [P, T2], U8) for g in range(2)]
        y_late = tile("y_late", [P, 2, PACK, BANK], F32, "slot2")
        for c in range(2):
            for g in range(2):
                y = tile("y%d" % g, [P, PACK, BANK], F32, "slot%d" % g)[:] if c == 0 else y_late[:, g]
                for t in range(PACK):
                    n = PACK * g + t
                    if c == 0:
                        acc = early[n]
                    else:
                        acc = bank("y_1_%d" % n, n)
                        product(acc, 0, n, c)
                    product(acc, 1, n, c)
                    nc.scalar.copy(y[:, t, :], acc[:])
                    nc.sync.dma_start(out_rows[g][:, t, chunks[c]], y[:, t, :])
                yb = tile("yb%d%d" % (c, g), [P, WIDE], BF16, ("bfB", "spb", "spa", "bfB")[2 * c + g])
                interleave(nc.vector.tensor_copy, yb[:], y)
                codes = tile("y_codes%d%d" % (c, g), [P, BANK], U32)
                nc.vector.quantize_mx(out=codes[:].bitcast(E4M3), scales=y_scales[g][:, chunks[c]], in_=yb[:])
                words = out_1[g].rearrange("p m t -> p (m t)").bitcast(I32)
                nc.sync.dma_start(words[:, chunks[c]], codes[:].bitcast(I32))
                if c == 1:
                    for q in range(4):
                        nc.sync.dma_start(
                            out_2[g][4 * q : 4 * q + 4, :].bitcast(I32),
                            y_scales[g][32 * q : 32 * q + 4, :].bitcast(I32),
                        )
